import numpy as np
import ml_dtypes


def mxq(x, axis, fmt="e4m3"):
    dtype, down = {"e4m3": (ml_dtypes.float8_e4m3fn, 7), "e5m2": (ml_dtypes.float8_e5m2, 14)}[fmt]
    v = np.moveaxis(np.asarray(x, np.float32).astype(ml_dtypes.bfloat16).astype(np.float64), axis, -1)
    blocks = v.reshape(v.shape[:-1] + (-1, 32))
    amax = np.abs(blocks).max(-1, keepdims=True)
    byte = np.maximum(np.where(amax > 0, np.frexp(amax)[1] - 1 + 127, 0) - down, 1)
    scale = np.exp2(byte - 127.0)
    codes = (blocks / scale).astype(np.float32).astype(dtype).astype(np.float64)
    return np.moveaxis((codes * scale).reshape(v.shape), -1, axis)


WIDE = False


def mx_kscale(k):
    if not WIDE:
        return np.ones(k)
    levels = np.array([10, -10, 5, -5, 0])
    if k % 512:
        return np.exp2(np.random.permutation(np.resize(levels, k // 32))).repeat(32)
    a = np.empty((k // 512, 16))
    for p in range(k // 512):
        a[p, :8] = np.random.permutation(np.resize(levels, 8))
        for g in range(8):
            far = levels[np.abs(levels - a[p, g]) >= 10]
            a[p, g + 8] = far[np.random.randint(len(far))]
    return np.exp2(a.ravel()).repeat(32)


def f64(x):
    return np.asarray(x).astype(np.float64)


def striped(idx):
    return np.tile(idx.reshape(-1, 16).T, (8, 1)).astype(np.uint16)


def unstriped(offs):
    return offs[:16].T.reshape(-1).astype(np.int64)


E2M1 = np.array([0.0, 0.5, 1.0, 1.5, 2.0, 3.0, 4.0, 6.0, -0.0, -0.5, -1.0, -1.5, -2.0, -3.0, -4.0, -6.0])


def pack_weight(w, fmt):
    k, n = w.shape
    w = f64(np.asarray(w, np.float32).astype(ml_dtypes.bfloat16)).reshape(k // 32, 32, n)
    amax = np.abs(w).max(1)
    if fmt == "e4m3":
        byte = np.frexp(amax)[1] - 1 + 127 - 7
    else:
        mant, ex = np.frexp(amax / 6.0)
        byte = np.where(mant > 0.5, ex, ex - 1) + 127
    byte = np.clip(np.where(amax > 0, byte, 1), 1, 254)
    scaled = (w * np.exp2(127.0 - byte)[:, None, :]).reshape(k, n).astype(np.float32)
    by_word = np.ascontiguousarray(scaled.reshape(k // 512, 128, 4, n).transpose(0, 1, 3, 2))
    if fmt == "e4m3":
        words = by_word.astype(ml_dtypes.float8_e4m3fn).view(np.uint8)
    else:
        c = by_word.astype(ml_dtypes.float4_e2m1fn).view(np.uint8) & 0xF
        words = (c[..., 0::2] | (c[..., 1::2] << 4)).reshape(k // 512, 128, 2 * n)
    return np.ascontiguousarray(words), np.ascontiguousarray(byte.astype(np.uint8).reshape(k // 512, 16, n))


def unpack_weight(words, scales, fmt):
    g, _, n = scales.shape
    words = np.ascontiguousarray(words).reshape(g, 128, n, -1)
    if fmt == "e4m3":
        vals = words.view(ml_dtypes.float8_e4m3fn).astype(np.float64)
    else:
        nib = np.empty((g, 128, n, 4), np.uint8)
        nib[..., 0::2] = words & 0xF
        nib[..., 1::2] = words >> 4
        vals = E2M1[nib]
    vals = vals * np.repeat(np.exp2(scales.astype(np.float64) - 127.0), 8, axis=1)[..., None]
    return vals.transpose(0, 1, 3, 2).reshape(g * 512, n)


def silu(v):
    return v / (1.0 + np.exp(-np.maximum(v, -700.0)))


K, T, E, C, H, N = 2048, 768, 4, 256, 512, 256


def by_expert(wq, xq):
    return np.concatenate([wq[e].T @ xq[:, e * C:(e + 1) * C] for e in range(E)], axis=1)


def setup_inputs():
    n = np.random.standard_normal
    s = mx_kscale(K)[:, None]
    u = mx_kscale(H)
    w1 = [pack_weight(m, "e2m1") for m in n((E, K, H)) / np.sqrt(K) / s[None] * u[None, None, :]]
    w2 = [pack_weight(m, "e2m1") for m in n((E, H, N)) / np.sqrt(H) / u[None, :, None]]
    idx = np.random.permutation(E * C)
    return {
        "xT": (n((K, T)) * s).astype(np.float32),
        "w1_words": np.stack([m[0] for m in w1]),
        "w1_scales": np.stack([m[1] for m in w1]),
        "w2_words": np.stack([m[0] for m in w2]),
        "w2_scales": np.stack([m[1] for m in w2]),
        "gate": np.tile(np.where(idx < T, np.random.uniform(0.2, 1.0, E * C), 0.0), (N, 1)).astype(np.float32),
        "offs": striped(idx),
    }


def reference(xT, w1_words, w1_scales, w2_words, w2_scales, gate, offs):
    idx = unstriped(offs)
    w1 = np.stack([unpack_weight(w1_words[e], w1_scales[e], "e2m1") for e in range(E)])
    w2 = np.stack([unpack_weight(w2_words[e], w2_scales[e], "e2m1") for e in range(E)])
    xq = mxq(np.concatenate([f64(xT), np.zeros((K, E * C - T))], axis=1)[:, idx], 0, "e4m3")
    h = silu(by_expert(w1, xq))
    y = by_expert(w2, mxq(h, 0, "e4m3"))
    out = np.zeros((N, E * C))
    out[:, idx] = f64(gate) * y
    return out[:, :T]

@@ -1,0 +1,215 @@
+from contextlib import ExitStack
+
+import concourse.mybir as mybir
+from concourse.masks import make_identity
+
+K, T, E, C, H, N = 2048, 768, 4, 256, 512, 256
+S = E * C
+FLOPS = 2 * S * (K * H + H * N)
+
+F32 = mybir.dt.float32
+BF16 = mybir.dt.bfloat16
+I32 = mybir.dt.int32
+U32 = mybir.dt.uint32
+U16 = mybir.dt.uint16
+U8 = mybir.dt.uint8
+FP8X4 = mybir.dt.float8_e4m3fn_x4
+FP4X4 = mybir.dt.float4_e2m1fn_x4
+ACT = mybir.ActivationFunctionType
+MULT = mybir.AluOpType.mult
+
+P = 128
+PACK = 4
+PASSES = K // (P * PACK)
+LIST_COLS = C // 16
+N_HALVES = N // P
+SLOT_TILES = C // P
+LAST = PASSES - 1
+MOVED_ROWS = 112
+
+X_LOADS = [[(0, 256), (256, 768)], [(0, 768)], [(0, 512), (512, 768)], [(0, 512), (512, 768)]]
+X_COPIES = [
+    [(0, 256, "dve"), (256, 512, "act"), (512, 768, "dve")],
+    [(0, 512, "act"), (512, 768, "dve")],
+    [(0, 512, "act"), (512, 768, "act")],
+    [(0, 512, "act"), (512, 768, "act")],
+]
+
+
+def tile_moe_pad_mlp_silu_kernel(
+    tc, xT, w1_words, w1_scales, w2_words, w2_scales, gate, offs, out
+):
+    nc = tc.nc
+    with ExitStack() as ctx:
+        keep = ctx.enter_context(tc.tile_pool(name="keep", bufs=1))
+        psum = ctx.enter_context(tc.psum_pool(name="psum", bufs=1))
+
+        offsets = keep.tile([P, S // 16], U16, name="offsets")
+        nc.sync.dma_start(offsets[:], offs)
+
+        tok_words = keep.tile([P, PASSES, S], I32, name="tok_words", align_bytes=64)
+        tok_bytes = keep.tile([P, 2, S], U8, name="tok_bytes", align_bytes=64)
+        slot_words = [keep.tile([P, S], U32, name=f"slot_words{s}", align_bytes=64) for s in range(PASSES)]
+        slot_bytes = [keep.tile([P, S], U8, name=f"slot_bytes{i}", align_bytes=64) for i in range(2)]
+        moved_bytes = keep.tile([P, 2, S], U8, name="moved_bytes", align_bytes=64)
+        w1_plane = keep.tile([P, E * PASSES, H], U8, name="w1_plane", align_bytes=64)
+        w2_plane = keep.tile([P, E, N], U8, name="w2_plane", align_bytes=64)
+        w1_codes = [keep.tile([P, PASSES, 2 * H], U8, name=f"w1_codes{e}", align_bytes=64) for e in range(E)]
+        w2_codes = keep.tile([P, E, 2 * N], U8, name="w2_codes", align_bytes=64)
+        gates = keep.tile([P, N_HALVES, S], F32, name="gates")
+        ident = keep.tile([P, P], F32, name="ident")
+
+        nc.vector.memset(tok_bytes[:].bitcast(I32), 0)
+        nc.vector.memset(tok_words[:, :, T:S], 0)
+        nc.gpsimd.memset(w1_plane[:].bitcast(I32), 0)
+        nc.gpsimd.memset(w2_plane[:].bitcast(I32), 0)
+        nc.gpsimd.memset(moved_bytes[:].bitcast(I32), 0)
+        make_identity(nc, ident[:])
+
+        raw = {}
+
+        def load_x(s):
+            rows = xT[s * P * PACK : (s + 1) * P * PACK, :].rearrange("(p j) w -> p j w", j=PACK)
+            for t0, t1 in X_LOADS[s]:
+                chunk = keep.tile([P, PACK, t1 - t0], F32, name=f"x_raw{s}_{t0}")
+                nc.sync.dma_start(out=chunk[:], in_=rows[:, :, t0:t1])
+                raw[(s, t0)] = chunk
+
+        def load_plane(plane, scales, c0, c1):
+            by_row = scales.rearrange("e s (q r) n -> r q (e s) n", r=4)
+            for r in range(4):
+                nc.sync.dma_start(out=plane[r:P:32, c0:c1, :].bitcast(I32), in_=by_row[r][:, c0:c1, :].bitcast(I32))
+
+        def load_w1(e):
+            nc.sync.dma_start(
+                out=w1_codes[e][:].bitcast(I32), in_=w1_words[e].rearrange("s p b -> p s b").bitcast(I32)
+            )
+
+        for s in range(PASSES):
+            load_x(s)
+        load_plane(w1_plane, w1_scales, 0, PASSES)
+        load_w1(0)
+        load_plane(w1_plane, w1_scales, PASSES, E * PASSES)
+        load_w1(1)
+        load_plane(w2_plane, w2_scales, 0, E)
+        nc.sync.dma_start(
+            out=w2_codes[:].bitcast(I32), in_=w2_words.rearrange("e s p b -> p (e s) b").bitcast(I32)
+        )
+        nc.sync.dma_start(out=gates[:], in_=gate.rearrange("(h p) j -> p h j", p=P))
+        load_w1(2)
+        load_w1(3)
+
+        for s in range(PASSES):
+            grouped = keep.tile([P, T, PACK], BF16, name=f"x_grouped{s}", align_bytes=64)
+            for t0, t1, engine in X_COPIES[s]:
+                l0 = max(a for a, b in X_LOADS[s] if a <= t0)
+                src = raw[(s, l0)][:, :, t0 - l0 : t1 - l0].rearrange("p t (c i) -> p c t i", i=4)
+                dst = grouped[:, t0:t1, :].rearrange("p (c i) t -> p c t i", i=4)
+                if engine == "act":
+                    nc.scalar.activation(out=dst, in_=src, func=ACT.Copy)
+                else:
+                    nc.vector.tensor_copy(out=dst, in_=src)
+                nc.vector.quantize_mx(
+                    out=tok_words[:, s, t0:t1].bitcast(FP8X4),
+                    scales=tok_bytes[4 * s : P, 0, t0:t1] if s < LAST else tok_bytes[:, 1, t0:t1],
+                    in_=grouped[:, t0:t1, :].rearrange("p w t -> p (w t)"),
+                )
+
+        def expert_list(e):
+            return offsets[:, e * LIST_COLS : (e + 1) * LIST_COLS]
+
+        def gather_words(s, c0, c1):
+            nc.vector.tensor_copy(
+                slot_words[s][:, c0:c1], tok_words[:, s, :].bitcast(U32).indirect(offsets[:, c0 // 16 : c1 // 16])
+            )
+
+        def gather_bytes(i, c0, c1):
+            nc.vector.tensor_copy(slot_bytes[i][:, c0:c1], tok_bytes[:, i, :].indirect(offsets[:, c0 // 16 : c1 // 16]))
+
+        def gather_shared_bytes(c0, c1):
+            gather_bytes(0, c0, c1)
+            for s in range(1, LAST):
+                nc.gpsimd.dma_start(
+                    out=moved_bytes[0:MOVED_ROWS, s - 1, c0:c1].bitcast(I32),
+                    in_=slot_bytes[0][4 * s : 4 * s + MOVED_ROWS, c0:c1].bitcast(I32),
+                )
+
+        gather_shared_bytes(0, C)
+        for s in range(LAST - 1):
+            gather_words(s, 0, 2 * C)
+        gather_words(LAST - 1, 0, C)
+        gather_shared_bytes(C, S)
+        for e in range(E):
+            if e == 2:
+                for s in range(LAST - 1):
+                    gather_words(s, 2 * C, S)
+            if e > 0:
+                gather_words(LAST - 1, e * C, (e + 1) * C)
+            gather_bytes(1, e * C, (e + 1) * C)
+            gather_words(LAST, e * C, (e + 1) * C)
+
+        def slot_plane(s, cols):
+            if s == 0:
+                return slot_bytes[0][:, cols]
+            if s == LAST:
+                return slot_bytes[1][:, cols]
+            return moved_bytes[:, s - 1, cols]
+
+        results = []
+        for e in range(E):
+            turned = psum.tile([P, SLOT_TILES, 2, P], F32, name="turned", tag="turned", bufs=2)
+            for j in range(SLOT_TILES):
+                cols = slice(e * C + j * P, e * C + (j + 1) * P)
+                acc = psum.tile([P, H], F32, name="acc", tag="acc", bufs=4)
+                for s in range(PASSES):
+                    nc.tensor.matmul_mx(
+                        out=acc[:],
+                        lhsT=slot_words[s][:, cols].bitcast(FP8X4),
+                        lhsT_scale=slot_plane(s, cols),
+                        rhs=w1_codes[e][:, s, :].bitcast(FP4X4),
+                        rhs_scale=w1_plane[:, e * PASSES + s, :],
+                        start=(s == 0),
+                        stop=(s == PASSES - 1),
+                    )
+                h_rows = keep.tile([P, H], BF16, name=f"h_rows{e}_{j}")
+                nc.scalar.activation(
+                    out=h_rows[:].rearrange("c (u p v) -> c u p v", u=2, v=2),
+                    in_=acc[:].rearrange("c (p u v) -> c u p v", u=2, v=2),
+                    func=ACT.Silu,
+                )
+                for u in range(2):
+                    nc.tensor.transpose(turned[:, j, u, :], h_rows[:].bitcast(F32)[:, u * P : (u + 1) * P], ident[:])
+            h_grouped = keep.tile([P, C * PACK], BF16, name=f"h_grouped{e}", align_bytes=64)
+            nc.scalar.copy(
+                out=h_grouped[:].bitcast(F32).rearrange("p (j c u) -> p j c u", j=SLOT_TILES, u=2),
+                in_=turned[:].rearrange("p j u c -> p j c u"),
+            )
+            h_words = keep.tile([P, C], U32, name=f"h_words{e}", align_bytes=64)
+            h_bytes = keep.tile([P, C], U8, name=f"h_bytes{e}", align_bytes=64)
+            nc.vector.quantize_mx(out=h_words[:].bitcast(FP8X4), scales=h_bytes[:], in_=h_grouped[:])
+            y_acc = psum.tile([P, N_HALVES, C], F32, name="y_acc", tag="y_acc", bufs=2)
+            for half in range(N_HALVES):
+                nc.tensor.matmul_mx(
+                    out=y_acc[:, half, :],
+                    lhsT=w2_codes[:, e, half * 2 * P : (half + 1) * 2 * P].bitcast(FP4X4),
+                    lhsT_scale=w2_plane[:, e, half * P : (half + 1) * P],
+                    rhs=h_words[:].bitcast(FP8X4),
+                    rhs_scale=h_bytes[:],
+                    start=True,
+                    stop=True,
+                )
+            y = keep.tile([P, N_HALVES, C], F32, name=f"y{e}")
+            nc.scalar.copy(out=y[:], in_=y_acc[:])
+            results.append(y)
+
+        windows = [keep.tile([P, S], F32, name=f"window{half}") for half in range(N_HALVES)]
+        for e in range(E):
+            for half in range(N_HALVES):
+                nc.vector.tensor_tensor(
+                    windows[half][:].indirect(expert_list(e)),
+                    results[e][:, half, :],
+                    gates[:, half, e * C : (e + 1) * C],
+                    MULT,
+                )
+        for half in range(N_HALVES):
+            nc.sync.dma_start(out=out[half * P : (half + 1) * P, :], in_=windows[half][:, 0:T])

@@ -54,9 +54,8 @@ def tile_moe_pad_mlp_silu_kernel(
         moved_bytes = keep.tile([P, 2, S], U8, name="moved_bytes", align_bytes=64)
         w1_plane = keep.tile([P, E * PASSES, H], U8, name="w1_plane", align_bytes=64)
         w2_plane = keep.tile([P, E, N], U8, name="w2_plane", align_bytes=64)
-        w1_codes = [keep.tile([P, PASSES, 2 * H], U8, name=f"w1_codes{e}", align_bytes=64) for e in range(E)]
+        w1_early = [keep.tile([P, PASSES, 2 * H], U8, name=f"w1_early{e}", align_bytes=64) for e in range(2)]
         w2_codes = keep.tile([P, E, 2 * N], U8, name="w2_codes", align_bytes=64)
-        gates = keep.tile([P, N_HALVES, S], F32, name="gates")
         ident = keep.tile([P, P], F32, name="ident")
 
         nc.vector.memset(tok_bytes[:].bitcast(I32), 0)
@@ -71,33 +70,29 @@ def tile_moe_pad_mlp_silu_kernel(
         def load_x(s):
             rows = xT[s * P * PACK : (s + 1) * P * PACK, :].rearrange("(p j) w -> p j w", j=PACK)
             for t0, t1 in X_LOADS[s]:
-                chunk = keep.tile([P, PACK, t1 - t0], F32, name=f"x_raw{s}_{t0}")
+                chunk = keep.tile([P, PACK, t1 - t0], F32, name=f"x_raw{s}_{t0}", align_bytes=64)
                 nc.sync.dma_start(out=chunk[:], in_=rows[:, :, t0:t1])
                 raw[(s, t0)] = chunk
 
-        def load_plane(plane, scales, c0, c1):
+        def load_plane(queue, plane, scales):
             by_row = scales.rearrange("e s (q r) n -> r q (e s) n", r=4)
             for r in range(4):
-                nc.sync.dma_start(out=plane[r:P:32, c0:c1, :].bitcast(I32), in_=by_row[r][:, c0:c1, :].bitcast(I32))
+                queue.dma_start(out=plane[r:P:32, :, :].bitcast(I32), in_=by_row[r].bitcast(I32))
 
         def load_w1(e):
             nc.sync.dma_start(
-                out=w1_codes[e][:].bitcast(I32), in_=w1_words[e].rearrange("s p b -> p s b").bitcast(I32)
+                out=w1_early[e][:].bitcast(I32), in_=w1_words[e].rearrange("s p b -> p s b").bitcast(I32)
             )
 
         for s in range(PASSES):
             load_x(s)
-        load_plane(w1_plane, w1_scales, 0, PASSES)
+        load_plane(nc.sync, w1_plane, w1_scales)
         load_w1(0)
-        load_plane(w1_plane, w1_scales, PASSES, E * PASSES)
         load_w1(1)
-        load_plane(w2_plane, w2_scales, 0, E)
+        load_plane(nc.gpsimd, w2_plane, w2_scales)
         nc.sync.dma_start(
             out=w2_codes[:].bitcast(I32), in_=w2_words.rearrange("e s p b -> p (e s) b").bitcast(I32)
         )
-        nc.sync.dma_start(out=gates[:], in_=gate.rearrange("(h p) j -> p h j", p=P))
-        load_w1(2)
-        load_w1(3)
 
         for s in range(PASSES):
             grouped = keep.tile([P, T, PACK], BF16, name=f"x_grouped{s}", align_bytes=64)
@@ -129,16 +124,29 @@ def tile_moe_pad_mlp_silu_kernel(
         def gather_shared_bytes(c0, c1):
             gather_bytes(0, c0, c1)
             for s in range(1, LAST):
-                nc.gpsimd.dma_start(
+                nc.scalar.dma_start(
                     out=moved_bytes[0:MOVED_ROWS, s - 1, c0:c1].bitcast(I32),
                     in_=slot_bytes[0][4 * s : 4 * s + MOVED_ROWS, c0:c1].bitcast(I32),
                 )
 
-        gather_shared_bytes(0, C)
+        gather_shared_bytes(0, 2 * C)
+        gather_shared_bytes(2 * C, S)
+
+        w1_late = keep.tile([P, 2, PASSES, 2 * H], U8, name="w1_late", tag=f"x_raw{LAST}_0", align_bytes=64)
+        gates = [
+            keep.tile([P, S], F32, name="gates0", tag=f"x_raw{LAST}_512", align_bytes=64),
+            keep.tile([P, S], F32, name="gates1", tag=f"x_grouped{LAST}", align_bytes=64),
+        ]
+        nc.sync.dma_start(
+            out=w1_late[:].bitcast(I32), in_=w1_words[2:E].rearrange("e s p b -> p e s b").bitcast(I32)
+        )
+        for half in range(N_HALVES):
+            nc.sync.dma_start(out=gates[half][:], in_=gate[half * P : (half + 1) * P, :])
+        w1_codes = [w1_early[0][:], w1_early[1][:], w1_late[:, 0], w1_late[:, 1]]
+
         for s in range(LAST - 1):
             gather_words(s, 0, 2 * C)
         gather_words(LAST - 1, 0, C)
-        gather_shared_bytes(C, S)
         for e in range(E):
             if e == 2:
                 for s in range(LAST - 1):
@@ -155,12 +163,14 @@ def tile_moe_pad_mlp_silu_kernel(
                 return slot_bytes[1][:, cols]
             return moved_bytes[:, s - 1, cols]
 
-        results = []
-        for e in range(E):
-            turned = psum.tile([P, SLOT_TILES, 2, P], F32, name="turned", tag="turned", bufs=2)
+        windows = [keep.tile([P, S], F32, name=f"window{half}") for half in range(N_HALVES)]
+        hidden = {}
+
+        def first_layer(e):
+            turned = psum.tile([P, SLOT_TILES, 2, P], F32, name="turned", tag=f"small{e % 2}")
             for j in range(SLOT_TILES):
                 cols = slice(e * C + j * P, e * C + (j + 1) * P)
-                acc = psum.tile([P, H], F32, name="acc", tag="acc", bufs=4)
+                acc = psum.tile([P, H], F32, name="acc", tag="acc", bufs=6)
                 for s in range(PASSES):
                     nc.tensor.matmul_mx(
                         out=acc[:],
@@ -187,7 +197,11 @@ def tile_moe_pad_mlp_silu_kernel(
             h_words = keep.tile([P, C], U32, name=f"h_words{e}", align_bytes=64)
             h_bytes = keep.tile([P, C], U8, name=f"h_bytes{e}", align_bytes=64)
             nc.vector.quantize_mx(out=h_words[:].bitcast(FP8X4), scales=h_bytes[:], in_=h_grouped[:])
-            y_acc = psum.tile([P, N_HALVES, C], F32, name="y_acc", tag="y_acc", bufs=2)
+            hidden[e] = (h_words, h_bytes)
+
+        def second_layer(e):
+            h_words, h_bytes = hidden[e]
+            y_acc = psum.tile([P, N_HALVES, C], F32, name="y_acc", tag=f"small{(e + 1) % 2}")
             for half in range(N_HALVES):
                 nc.tensor.matmul_mx(
                     out=y_acc[:, half, :],
@@ -200,16 +214,18 @@ def tile_moe_pad_mlp_silu_kernel(
                 )
             y = keep.tile([P, N_HALVES, C], F32, name=f"y{e}")
             nc.scalar.copy(out=y[:], in_=y_acc[:])
-            results.append(y)
-
-        windows = [keep.tile([P, S], F32, name=f"window{half}") for half in range(N_HALVES)]
-        for e in range(E):
             for half in range(N_HALVES):
                 nc.vector.tensor_tensor(
                     windows[half][:].indirect(expert_list(e)),
-                    results[e][:, half, :],
-                    gates[:, half, e * C : (e + 1) * C],
+                    y[:, half, :],
+                    gates[half][:, e * C : (e + 1) * C],
                     MULT,
                 )
+
+        first_layer(0)
+        for e in range(1, E):
+            first_layer(e)
+            second_layer(e - 1)
+        second_layer(E - 1)
         for half in range(N_HALVES):
             nc.sync.dma_start(out=out[half * P : (half + 1) * P, :], in_=windows[half][:, 0:T])

@@ -26,8 +26,9 @@ N_HALVES = N // P
 SLOT_TILES = C // P
 LAST = PASSES - 1
 MOVED_ROWS = 112
+SUM_BANKS = 6
 
-X_LOADS = [[(0, 256), (256, 768)], [(0, 768)], [(0, 512), (512, 768)], [(0, 512), (512, 768)]]
+X_LOADS = [[(0, 256), (256, 768)], [(0, 512), (512, 768)], [(0, 512), (512, 768)], [(0, 512), (512, 768)]]
 X_COPIES = [
     [(0, 256, "dve"), (256, 512, "act"), (512, 768, "dve")],
     [(0, 512, "act"), (512, 768, "dve")],
@@ -49,7 +50,7 @@ def tile_moe_pad_mlp_silu_kernel(
 
         tok_words = keep.tile([P, PASSES, S], I32, name="tok_words", align_bytes=64)
         tok_bytes = keep.tile([P, 2, S], U8, name="tok_bytes", align_bytes=64)
-        slot_words = [keep.tile([P, S], U32, name=f"slot_words{s}", align_bytes=64) for s in range(PASSES)]
+        slot_words = [keep.tile([P, S], U32, name=f"slot_words{s}", align_bytes=64) for s in range(2)]
         slot_bytes = [keep.tile([P, S], U8, name=f"slot_bytes{i}", align_bytes=64) for i in range(2)]
         moved_bytes = keep.tile([P, 2, S], U8, name="moved_bytes", align_bytes=64)
         w1_plane = keep.tile([P, E * PASSES, H], U8, name="w1_plane", align_bytes=64)
@@ -90,25 +91,28 @@ def tile_moe_pad_mlp_silu_kernel(
         load_w1(0)
         load_w1(1)
         load_plane(nc.gpsimd, w2_plane, w2_scales)
-        nc.sync.dma_start(
+        nc.gpsimd.dma_start(
             out=w2_codes[:].bitcast(I32), in_=w2_words.rearrange("e s p b -> p (e s) b").bitcast(I32)
         )
 
-        for s in range(PASSES):
-            grouped = keep.tile([P, T, PACK], BF16, name=f"x_grouped{s}", align_bytes=64)
-            for t0, t1, engine in X_COPIES[s]:
-                l0 = max(a for a, b in X_LOADS[s] if a <= t0)
-                src = raw[(s, l0)][:, :, t0 - l0 : t1 - l0].rearrange("p t (c i) -> p c t i", i=4)
-                dst = grouped[:, t0:t1, :].rearrange("p (c i) t -> p c t i", i=4)
-                if engine == "act":
-                    nc.scalar.activation(out=dst, in_=src, func=ACT.Copy)
-                else:
-                    nc.vector.tensor_copy(out=dst, in_=src)
-                nc.vector.quantize_mx(
-                    out=tok_words[:, s, t0:t1].bitcast(FP8X4),
-                    scales=tok_bytes[4 * s : P, 0, t0:t1] if s < LAST else tok_bytes[:, 1, t0:t1],
-                    in_=grouped[:, t0:t1, :].rearrange("p w t -> p (w t)"),
-                )
+        def quantize_tokens(s, t0, t1, engine):
+            grouped = keep.tile([P, t1 - t0, PACK], BF16, name=f"x_grouped{s}_{t0}", align_bytes=64)
+            l0 = max(a for a, b in X_LOADS[s] if a <= t0)
+            src = raw[(s, l0)][:, :, t0 - l0 : t1 - l0].rearrange("p t (c i) -> p c t i", i=4)
+            dst = grouped[:].rearrange("p (c i) t -> p c t i", i=4)
+            if engine == "act":
+                nc.scalar.activation(out=dst, in_=src, func=ACT.Copy)
+            else:
+                nc.vector.tensor_copy(out=dst, in_=src)
+            nc.vector.quantize_mx(
+                out=tok_words[:, s, t0:t1].bitcast(FP8X4),
+                scales=tok_bytes[4 * s : P, 0, t0:t1] if s < LAST else tok_bytes[:, 1, t0:t1],
+                in_=grouped[:].rearrange("p w t -> p (w t)"),
+            )
+
+        for s in range(LAST):
+            for piece in X_COPIES[s]:
+                quantize_tokens(s, *piece)
 
         def expert_list(e):
             return offsets[:, e * LIST_COLS : (e + 1) * LIST_COLS]
@@ -121,40 +125,55 @@ def tile_moe_pad_mlp_silu_kernel(
         def gather_bytes(i, c0, c1):
             nc.vector.tensor_copy(slot_bytes[i][:, c0:c1], tok_bytes[:, i, :].indirect(offsets[:, c0 // 16 : c1 // 16]))
 
-        def gather_shared_bytes(c0, c1):
+        def gather_shared_bytes(queue, c0, c1):
             gather_bytes(0, c0, c1)
             for s in range(1, LAST):
-                nc.scalar.dma_start(
+                queue.dma_start(
                     out=moved_bytes[0:MOVED_ROWS, s - 1, c0:c1].bitcast(I32),
                     in_=slot_bytes[0][4 * s : 4 * s + MOVED_ROWS, c0:c1].bitcast(I32),
                 )
 
-        gather_shared_bytes(0, 2 * C)
-        gather_shared_bytes(2 * C, S)
+        gather_shared_bytes(nc.scalar, 0, 2 * C)
+        gather_shared_bytes(nc.scalar, 2 * C, S)
+        for piece in X_COPIES[LAST]:
+            quantize_tokens(LAST, *piece)
 
-        w1_late = keep.tile([P, 2, PASSES, 2 * H], U8, name="w1_late", tag=f"x_raw{LAST}_0", align_bytes=64)
-        gates = [
-            keep.tile([P, S], F32, name="gates0", tag=f"x_raw{LAST}_512", align_bytes=64),
-            keep.tile([P, S], F32, name="gates1", tag=f"x_grouped{LAST}", align_bytes=64),
-        ]
-        nc.sync.dma_start(
-            out=w1_late[:].bitcast(I32), in_=w1_words[2:E].rearrange("e s p b -> p e s b").bitcast(I32)
-        )
-        for half in range(N_HALVES):
-            nc.sync.dma_start(out=gates[half][:], in_=gate[half * P : (half + 1) * P, :])
-        w1_codes = [w1_early[0][:], w1_early[1][:], w1_late[:, 0], w1_late[:, 1]]
+        w1_third = keep.tile([P, PASSES, 2 * H], U8, name="w1_third", tag=f"x_raw{LAST}_0", align_bytes=64)
+        w1_fourth = keep.tile([P, PASSES, 2 * H], U8, name="w1_fourth", tag=f"x_raw{LAST}_512", align_bytes=64)
+        gates = keep.tile([P, N_HALVES, S], F32, name="gates", tag=f"x_grouped{LAST}_0", align_bytes=64)
+        nc.sync.dma_start(out=w1_third[:].bitcast(I32), in_=w1_words[2].rearrange("s p b -> p s b").bitcast(I32))
+        nc.sync.dma_start(out=w1_fourth[:].bitcast(I32), in_=w1_words[3].rearrange("s p b -> p s b").bitcast(I32))
+        nc.sync.dma_start(out=gates[:], in_=gate.rearrange("(h p) j -> p h j", p=P))
+        w1_codes = [w1_early[0][:], w1_early[1][:], w1_third[:], w1_fourth[:]]
 
-        for s in range(LAST - 1):
-            gather_words(s, 0, 2 * C)
-        gather_words(LAST - 1, 0, C)
-        for e in range(E):
-            if e == 2:
-                for s in range(LAST - 1):
-                    gather_words(s, 2 * C, S)
-            if e > 0:
-                gather_words(LAST - 1, e * C, (e + 1) * C)
+        for s in range(2):
+            for c0 in range(0, S, 2 * C):
+                gather_words(s, c0, c0 + 2 * C)
+
+        late_words = {}
+
+        def gather_late_words(e, s, dst):
+            nc.vector.tensor_copy(dst, tok_words[:, s, :].bitcast(U32).indirect(expert_list(e)))
+            late_words[(e, s)] = dst
+
+        for e in range(3):
+            words = keep.tile([P, C], U32, name=f"late_words{e}_2", align_bytes=64)
+            gather_late_words(e, 2, words[:])
+        for e in range(3):
             gather_bytes(1, e * C, (e + 1) * C)
-            gather_words(LAST, e * C, (e + 1) * C)
+            words = keep.tile([P, C], U32, name=f"late_words{e}_3", align_bytes=64)
+            gather_late_words(e, LAST, words[:])
+        gather_bytes(1, 3 * C, S)
+
+        def gather_last_expert():
+            words = keep.tile([P, 2, C], U32, name="late_words3", tag="h_grouped0", align_bytes=64)
+            gather_late_words(3, 2, words[:, 0, :])
+            gather_late_words(3, LAST, words[:, 1, :])
+
+        def slot_codes(e, j, s):
+            if s < 2:
+                return slot_words[s][:, e * C + j * P : e * C + (j + 1) * P]
+            return late_words[(e, s)][:, j * P : (j + 1) * P]
 
         def slot_plane(s, cols):
             if s == 0:
@@ -166,21 +185,32 @@ def tile_moe_pad_mlp_silu_kernel(
         windows = [keep.tile([P, S], F32, name=f"window{half}") for half in range(N_HALVES)]
         hidden = {}
 
+        sums = {}
+
+        def first_pass(e, j, s):
+            cols = slice(e * C + j * P, e * C + (j + 1) * P)
+            nc.tensor.matmul_mx(
+                out=sums[(e, j)][:],
+                lhsT=slot_codes(e, j, s).bitcast(FP8X4),
+                lhsT_scale=slot_plane(s, cols),
+                rhs=w1_codes[e][:, s, :].bitcast(FP4X4),
+                rhs_scale=w1_plane[:, e * PASSES + s, :],
+                start=(s == 0),
+                stop=(s == LAST),
+            )
+
+        def open_sums(e):
+            for j in range(SLOT_TILES):
+                sums[(e, j)] = psum.tile([P, H], F32, name="acc", tag=f"sums{(e * SLOT_TILES + j) % SUM_BANKS}")
+                for s in range(LAST):
+                    first_pass(e, j, s)
+
         def first_layer(e):
             turned = psum.tile([P, SLOT_TILES, 2, P], F32, name="turned", tag=f"small{e % 2}")
             for j in range(SLOT_TILES):
-                cols = slice(e * C + j * P, e * C + (j + 1) * P)
-                acc = psum.tile([P, H], F32, name="acc", tag="acc", bufs=6)
-                for s in range(PASSES):
-                    nc.tensor.matmul_mx(
-                        out=acc[:],
-                        lhsT=slot_words[s][:, cols].bitcast(FP8X4),
-                        lhsT_scale=slot_plane(s, cols),
-                        rhs=w1_codes[e][:, s, :].bitcast(FP4X4),
-                        rhs_scale=w1_plane[:, e * PASSES + s, :],
-                        start=(s == 0),
-                        stop=(s == PASSES - 1),
-                    )
+                first_pass(e, j, LAST)
+            for j in range(SLOT_TILES):
+                acc = sums[(e, j)]
                 h_rows = keep.tile([P, H], BF16, name=f"h_rows{e}_{j}")
                 nc.scalar.activation(
                     out=h_rows[:].rearrange("c (u p v) -> c u p v", u=2, v=2),
@@ -199,33 +229,37 @@ def tile_moe_pad_mlp_silu_kernel(
             nc.vector.quantize_mx(out=h_words[:].bitcast(FP8X4), scales=h_bytes[:], in_=h_grouped[:])
             hidden[e] = (h_words, h_bytes)
 
-        def second_layer(e):
+        def second_layer(e, half):
             h_words, h_bytes = hidden[e]
-            y_acc = psum.tile([P, N_HALVES, C], F32, name="y_acc", tag=f"small{(e + 1) % 2}")
-            for half in range(N_HALVES):
-                nc.tensor.matmul_mx(
-                    out=y_acc[:, half, :],
-                    lhsT=w2_codes[:, e, half * 2 * P : (half + 1) * 2 * P].bitcast(FP4X4),
-                    lhsT_scale=w2_plane[:, e, half * P : (half + 1) * P],
-                    rhs=h_words[:].bitcast(FP8X4),
-                    rhs_scale=h_bytes[:],
-                    start=True,
-                    stop=True,
-                )
-            y = keep.tile([P, N_HALVES, C], F32, name=f"y{e}")
+            next_sums = min((e + 1) * SLOT_TILES, E * SLOT_TILES - 1) if e + 1 < E else E * SLOT_TILES - 1
+            bank = f"small{(e + 1) % 2}" if half else f"sums{next_sums % SUM_BANKS}"
+            y_acc = psum.tile([P, C], F32, name="y_acc", tag=bank)
+            nc.tensor.matmul_mx(
+                out=y_acc[:],
+                lhsT=w2_codes[:, e, half * 2 * P : (half + 1) * 2 * P].bitcast(FP4X4),
+                lhsT_scale=w2_plane[:, e, half * P : (half + 1) * P],
+                rhs=h_words[:].bitcast(FP8X4),
+                rhs_scale=h_bytes[:],
+                start=True,
+                stop=True,
+            )
+            y = keep.tile([P, C], F32, name=f"y{e}_{half}")
             nc.scalar.copy(out=y[:], in_=y_acc[:])
-            for half in range(N_HALVES):
-                nc.vector.tensor_tensor(
-                    windows[half][:].indirect(expert_list(e)),
-                    y[:, half, :],
-                    gates[half][:, e * C : (e + 1) * C],
-                    MULT,
-                )
+            nc.vector.tensor_tensor(
+                windows[half][:].indirect(expert_list(e)), y[:], gates[:, half, e * C : (e + 1) * C], MULT
+            )
 
+        open_sums(0)
+        open_sums(1)
         first_layer(0)
+        gather_last_expert()
         for e in range(1, E):
             first_layer(e)
-            second_layer(e - 1)
-        second_layer(E - 1)
+            for half in range(N_HALVES):
+                second_layer(e - 1, half)
+            if e + 1 < E:
+                open_sums(e + 1)
+        for half in range(N_HALVES):
+            second_layer(E - 1, half)
         for half in range(N_HALVES):
             nc.sync.dma_start(out=out[half * P : (half + 1) * P, :], in_=windows[half][:, 0:T])

@@ -54,16 +54,13 @@ def tile_moe_pad_mlp_silu_kernel(
         slot_bytes = [keep.tile([P, S], U8, name=f"slot_bytes{i}", align_bytes=64) for i in range(2)]
         moved_bytes = keep.tile([P, 2, S], U8, name="moved_bytes", align_bytes=64)
         w1_plane = keep.tile([P, E * PASSES, H], U8, name="w1_plane", align_bytes=64)
-        w2_plane = keep.tile([P, E, N], U8, name="w2_plane", align_bytes=64)
         w1_early = [keep.tile([P, PASSES, 2 * H], U8, name=f"w1_early{e}", align_bytes=64) for e in range(2)]
-        w2_codes = keep.tile([P, E, 2 * N], U8, name="w2_codes", align_bytes=64)
         ident = keep.tile([P, P], F32, name="ident")
 
         nc.vector.memset(tok_bytes[:].bitcast(I32), 0)
         nc.vector.memset(tok_words[:, :, T:S], 0)
-        nc.gpsimd.memset(w1_plane[:].bitcast(I32), 0)
-        nc.gpsimd.memset(w2_plane[:].bitcast(I32), 0)
-        nc.gpsimd.memset(moved_bytes[:].bitcast(I32), 0)
+        nc.vector.memset(w1_plane[:].bitcast(I32), 0)
+        nc.vector.memset(moved_bytes[:].bitcast(I32), 0)
         make_identity(nc, ident[:])
 
         raw = {}
@@ -90,10 +87,6 @@ def tile_moe_pad_mlp_silu_kernel(
         load_plane(nc.sync, w1_plane, w1_scales)
         load_w1(0)
         load_w1(1)
-        load_plane(nc.gpsimd, w2_plane, w2_scales)
-        nc.gpsimd.dma_start(
-            out=w2_codes[:].bitcast(I32), in_=w2_words.rearrange("e s p b -> p (e s) b").bitcast(I32)
-        )
 
         def quantize_tokens(s, t0, t1, engine):
             grouped = keep.tile([P, t1 - t0, PACK], BF16, name=f"x_grouped{s}_{t0}", align_bytes=64)
@@ -138,13 +131,19 @@ def tile_moe_pad_mlp_silu_kernel(
         for piece in X_COPIES[LAST]:
             quantize_tokens(LAST, *piece)
 
-        w1_third = keep.tile([P, PASSES, 2 * H], U8, name="w1_third", tag=f"x_raw{LAST}_0", align_bytes=64)
+        late_codes = keep.tile([P, PASSES + 2, 2 * H], U8, name="late_codes", tag=f"x_raw{LAST}_0", align_bytes=64)
+        w1_third = late_codes[:, 0:PASSES, :]
+        w2_codes = late_codes[:, PASSES:, :].rearrange("p a (b n) -> p (a b) n", b=2)
+        w2_plane = keep.tile([P, E, N], U8, name="w2_plane", tag=f"x_grouped{LAST}_0", align_bytes=64)
         w1_fourth = keep.tile([P, PASSES, 2 * H], U8, name="w1_fourth", tag=f"x_raw{LAST}_512", align_bytes=64)
-        gates = keep.tile([P, N_HALVES, S], F32, name="gates", tag=f"x_grouped{LAST}_0", align_bytes=64)
-        nc.sync.dma_start(out=w1_third[:].bitcast(I32), in_=w1_words[2].rearrange("s p b -> p s b").bitcast(I32))
+        gates = keep.tile([P, N_HALVES, S], F32, name="gates", tag=f"x_grouped{LAST}_512", align_bytes=64)
+        nc.sync.dma_start(out=w1_third.bitcast(I32), in_=w1_words[2].rearrange("s p b -> p s b").bitcast(I32))
+        nc.sync.dma_start(out=w2_codes.bitcast(I32), in_=w2_words.rearrange("e s p b -> p (e s) b").bitcast(I32))
+        nc.vector.memset(w2_plane[:].bitcast(I32), 0)
+        load_plane(nc.sync, w2_plane, w2_scales)
         nc.sync.dma_start(out=w1_fourth[:].bitcast(I32), in_=w1_words[3].rearrange("s p b -> p s b").bitcast(I32))
         nc.sync.dma_start(out=gates[:], in_=gate.rearrange("(h p) j -> p h j", p=P))
-        w1_codes = [w1_early[0][:], w1_early[1][:], w1_third[:], w1_fourth[:]]
+        w1_codes = [w1_early[0][:], w1_early[1][:], w1_third, w1_fourth[:]]
 
         for s in range(2):
             for c0 in range(0, S, 2 * C):

from contextlib import ExitStack

import concourse.mybir as mybir
from concourse.masks import make_identity

K, T, E, C, H, N = 2048, 768, 4, 256, 512, 256
S = E * C
FLOPS = 2 * S * (K * H + H * N)

F32 = mybir.dt.float32
BF16 = mybir.dt.bfloat16
I32 = mybir.dt.int32
U32 = mybir.dt.uint32
U16 = mybir.dt.uint16
U8 = mybir.dt.uint8
FP8X4 = mybir.dt.float8_e4m3fn_x4
FP4X4 = mybir.dt.float4_e2m1fn_x4
ACT = mybir.ActivationFunctionType
MULT = mybir.AluOpType.mult

P = 128
PACK = 4
PASSES = K // (P * PACK)
LIST_COLS = C // 16
N_HALVES = N // P
SLOT_TILES = C // P
LAST = PASSES - 1
MOVED_ROWS = 112
SUM_BANKS = 6

X_LOADS = [[(0, 256), (256, 768)], [(0, 512), (512, 768)], [(0, 512), (512, 768)], [(0, 512), (512, 768)]]
X_COPIES = [
    [(0, 256, "dve"), (256, 512, "act"), (512, 768, "dve")],
    [(0, 512, "act"), (512, 768, "dve")],
    [(0, 512, "act"), (512, 768, "act")],
    [(0, 512, "act"), (512, 768, "act")],
]


def tile_moe_pad_mlp_silu_kernel(
    tc, xT, w1_words, w1_scales, w2_words, w2_scales, gate, offs, out
):
    nc = tc.nc
    with ExitStack() as ctx:
        keep = ctx.enter_context(tc.tile_pool(name="keep", bufs=1))
        psum = ctx.enter_context(tc.psum_pool(name="psum", bufs=1))

        offsets = keep.tile([P, S // 16], U16, name="offsets")
        nc.sync.dma_start(offsets[:], offs)

        tok_words = keep.tile([P, PASSES, S], I32, name="tok_words", align_bytes=64)
        tok_bytes = keep.tile([P, 2, S], U8, name="tok_bytes", align_bytes=64)
        slot_words = [keep.tile([P, S], U32, name=f"slot_words{s}", align_bytes=64) for s in range(2)]
        slot_bytes = [keep.tile([P, S], U8, name=f"slot_bytes{i}", align_bytes=64) for i in range(2)]
        moved_bytes = keep.tile([P, 2, S], U8, name="moved_bytes", align_bytes=64)
        w1_plane = keep.tile([P, E * PASSES, H], U8, name="w1_plane", align_bytes=64)
        w1_early = [keep.tile([P, PASSES, 2 * H], U8, name=f"w1_early{e}", align_bytes=64) for e in range(2)]
        ident = keep.tile([P, P], F32, name="ident")

        nc.vector.memset(tok_bytes[:].bitcast(I32), 0)
        nc.vector.memset(tok_words[:, :, T:S], 0)
        nc.vector.memset(w1_plane[:].bitcast(I32), 0)
        nc.vector.memset(moved_bytes[:].bitcast(I32), 0)
        make_identity(nc, ident[:])

        raw = {}

        def load_x(s):
            rows = xT[s * P * PACK : (s + 1) * P * PACK, :].rearrange("(p j) w -> p j w", j=PACK)
            for t0, t1 in X_LOADS[s]:
                chunk = keep.tile([P, PACK, t1 - t0], F32, name=f"x_raw{s}_{t0}", align_bytes=64)
                nc.sync.dma_start(out=chunk[:], in_=rows[:, :, t0:t1])
                raw[(s, t0)] = chunk

        def load_plane(queue, plane, scales):
            by_row = scales.rearrange("e s (q r) n -> r q (e s) n", r=4)
            for r in range(4):
                queue.dma_start(out=plane[r:P:32, :, :].bitcast(I32), in_=by_row[r].bitcast(I32))

        def load_w1(e):
            nc.sync.dma_start(
                out=w1_early[e][:].bitcast(I32), in_=w1_words[e].rearrange("s p b -> p s b").bitcast(I32)
            )

        for s in range(PASSES):
            load_x(s)
        load_plane(nc.sync, w1_plane, w1_scales)
        load_w1(0)
        load_w1(1)

        def quantize_tokens(s, t0, t1, engine):
            grouped = keep.tile([P, t1 - t0, PACK], BF16, name=f"x_grouped{s}_{t0}", align_bytes=64)
            l0 = max(a for a, b in X_LOADS[s] if a <= t0)
            src = raw[(s, l0)][:, :, t0 - l0 : t1 - l0].rearrange("p t (c i) -> p c t i", i=4)
            dst = grouped[:].rearrange("p (c i) t -> p c t i", i=4)
            if engine == "act":
                nc.scalar.activation(out=dst, in_=src, func=ACT.Copy)
            else:
                nc.vector.tensor_copy(out=dst, in_=src)
            nc.vector.quantize_mx(
                out=tok_words[:, s, t0:t1].bitcast(FP8X4),
                scales=tok_bytes[4 * s : P, 0, t0:t1] if s < LAST else tok_bytes[:, 1, t0:t1],
                in_=grouped[:].rearrange("p w t -> p (w t)"),
            )

        for s in range(LAST):
            for piece in X_COPIES[s]:
                quantize_tokens(s, *piece)

        def expert_list(e):
            return offsets[:, e * LIST_COLS : (e + 1) * LIST_COLS]

        def gather_words(s, c0, c1):
            nc.vector.tensor_copy(
                slot_words[s][:, c0:c1], tok_words[:, s, :].bitcast(U32).indirect(offsets[:, c0 // 16 : c1 // 16])
            )

        def gather_bytes(i, c0, c1):
            nc.vector.tensor_copy(slot_bytes[i][:, c0:c1], tok_bytes[:, i, :].indirect(offsets[:, c0 // 16 : c1 // 16]))

        def gather_shared_bytes(queue, c0, c1):
            gather_bytes(0, c0, c1)
            for s in range(1, LAST):
                queue.dma_start(
                    out=moved_bytes[0:MOVED_ROWS, s - 1, c0:c1].bitcast(I32),
                    in_=slot_bytes[0][4 * s : 4 * s + MOVED_ROWS, c0:c1].bitcast(I32),
                )

        gather_shared_bytes(nc.scalar, 0, 2 * C)
        gather_shared_bytes(nc.scalar, 2 * C, S)
        for piece in X_COPIES[LAST]:
            quantize_tokens(LAST, *piece)

        late_codes = keep.tile([P, PASSES + 2, 2 * H], U8, name="late_codes", tag=f"x_raw{LAST}_0", align_bytes=64)
        w1_third = late_codes[:, 0:PASSES, :]
        w2_codes = late_codes[:, PASSES:, :].rearrange("p a (b n) -> p (a b) n", b=2)
        w2_plane = keep.tile([P, E, N], U8, name="w2_plane", tag=f"x_grouped{LAST}_0", align_bytes=64)
        w1_fourth = keep.tile([P, PASSES, 2 * H], U8, name="w1_fourth", tag=f"x_raw{LAST}_512", align_bytes=64)
        gates = keep.tile([P, N_HALVES, S], F32, name="gates", tag=f"x_grouped{LAST}_512", align_bytes=64)
        nc.sync.dma_start(out=w1_third.bitcast(I32), in_=w1_words[2].rearrange("s p b -> p s b").bitcast(I32))
        nc.sync.dma_start(out=w2_codes.bitcast(I32), in_=w2_words.rearrange("e s p b -> p (e s) b").bitcast(I32))
        nc.vector.memset(w2_plane[:].bitcast(I32), 0)
        load_plane(nc.sync, w2_plane, w2_scales)
        nc.sync.dma_start(out=w1_fourth[:].bitcast(I32), in_=w1_words[3].rearrange("s p b -> p s b").bitcast(I32))
        nc.sync.dma_start(out=gates[:], in_=gate.rearrange("(h p) j -> p h j", p=P))
        w1_codes = [w1_early[0][:], w1_early[1][:], w1_third, w1_fourth[:]]

        for s in range(2):
            for c0 in range(0, S, 2 * C):
                gather_words(s, c0, c0 + 2 * C)

        late_words = {}

        def gather_late_words(e, s, dst):
            nc.vector.tensor_copy(dst, tok_words[:, s, :].bitcast(U32).indirect(expert_list(e)))
            late_words[(e, s)] = dst

        for e in range(3):
            words = keep.tile([P, C], U32, name=f"late_words{e}_2", align_bytes=64)
            gather_late_words(e, 2, words[:])
        for e in range(3):
            gather_bytes(1, e * C, (e + 1) * C)
            words = keep.tile([P, C], U32, name=f"late_words{e}_3", align_bytes=64)
            gather_late_words(e, LAST, words[:])
        gather_bytes(1, 3 * C, S)

        def gather_last_expert():
            words = keep.tile([P, 2, C], U32, name="late_words3", tag="h_grouped0", align_bytes=64)
            gather_late_words(3, 2, words[:, 0, :])
            gather_late_words(3, LAST, words[:, 1, :])

        def slot_codes(e, j, s):
            if s < 2:
                return slot_words[s][:, e * C + j * P : e * C + (j + 1) * P]
            return late_words[(e, s)][:, j * P : (j + 1) * P]

        def slot_plane(s, cols):
            if s == 0:
                return slot_bytes[0][:, cols]
            if s == LAST:
                return slot_bytes[1][:, cols]
            return moved_bytes[:, s - 1, cols]

        windows = [keep.tile([P, S], F32, name=f"window{half}") for half in range(N_HALVES)]
        hidden = {}

        sums = {}

        def first_pass(e, j, s):
            cols = slice(e * C + j * P, e * C + (j + 1) * P)
            nc.tensor.matmul_mx(
                out=sums[(e, j)][:],
                lhsT=slot_codes(e, j, s).bitcast(FP8X4),
                lhsT_scale=slot_plane(s, cols),
                rhs=w1_codes[e][:, s, :].bitcast(FP4X4),
                rhs_scale=w1_plane[:, e * PASSES + s, :],
                start=(s == 0),
                stop=(s == LAST),
            )

        def open_sums(e):
            for j in range(SLOT_TILES):
                sums[(e, j)] = psum.tile([P, H], F32, name="acc", tag=f"sums{(e * SLOT_TILES + j) % SUM_BANKS}")
                for s in range(LAST):
                    first_pass(e, j, s)

        def first_layer(e):
            turned = psum.tile([P, SLOT_TILES, 2, P], F32, name="turned", tag=f"small{e % 2}")
            for j in range(SLOT_TILES):
                first_pass(e, j, LAST)
            for j in range(SLOT_TILES):
                acc = sums[(e, j)]
                h_rows = keep.tile([P, H], BF16, name=f"h_rows{e}_{j}")
                nc.scalar.activation(
                    out=h_rows[:].rearrange("c (u p v) -> c u p v", u=2, v=2),
                    in_=acc[:].rearrange("c (p u v) -> c u p v", u=2, v=2),
                    func=ACT.Silu,
                )
                for u in range(2):
                    nc.tensor.transpose(turned[:, j, u, :], h_rows[:].bitcast(F32)[:, u * P : (u + 1) * P], ident[:])
            h_grouped = keep.tile([P, C * PACK], BF16, name=f"h_grouped{e}", align_bytes=64)
            nc.scalar.copy(
                out=h_grouped[:].bitcast(F32).rearrange("p (j c u) -> p j c u", j=SLOT_TILES, u=2),
                in_=turned[:].rearrange("p j u c -> p j c u"),
            )
            h_words = keep.tile([P, C], U32, name=f"h_words{e}", align_bytes=64)
            h_bytes = keep.tile([P, C], U8, name=f"h_bytes{e}", align_bytes=64)
            nc.vector.quantize_mx(out=h_words[:].bitcast(FP8X4), scales=h_bytes[:], in_=h_grouped[:])
            hidden[e] = (h_words, h_bytes)

        def second_layer(e, half):
            h_words, h_bytes = hidden[e]
            next_sums = min((e + 1) * SLOT_TILES, E * SLOT_TILES - 1) if e + 1 < E else E * SLOT_TILES - 1
            bank = f"small{(e + 1) % 2}" if half else f"sums{next_sums % SUM_BANKS}"
            y_acc = psum.tile([P, C], F32, name="y_acc", tag=bank)
            nc.tensor.matmul_mx(
                out=y_acc[:],
                lhsT=w2_codes[:, e, half * 2 * P : (half + 1) * 2 * P].bitcast(FP4X4),
                lhsT_scale=w2_plane[:, e, half * P : (half + 1) * P],
                rhs=h_words[:].bitcast(FP8X4),
                rhs_scale=h_bytes[:],
                start=True,
                stop=True,
            )
            y = keep.tile([P, C], F32, name=f"y{e}_{half}")
            nc.scalar.copy(out=y[:], in_=y_acc[:])
            nc.vector.tensor_tensor(
                windows[half][:].indirect(expert_list(e)), y[:], gates[:, half, e * C : (e + 1) * C], MULT
            )

        open_sums(0)
        open_sums(1)
        first_layer(0)
        gather_last_expert()
        for e in range(1, E):
            first_layer(e)
            for half in range(N_HALVES):
                second_layer(e - 1, half)
            if e + 1 < E:
                open_sums(e + 1)
        for half in range(N_HALVES):
            second_layer(E - 1, half)
        for half in range(N_HALVES):
            nc.sync.dma_start(out=out[half * P : (half + 1) * P, :], in_=windows[half][:, 0:T])
